import numpy as np
import ml_dtypes


def mxq(x, axis, fmt="e4m3"):
    dtype, down = {"e4m3": (ml_dtypes.float8_e4m3fn, 7), "e5m2": (ml_dtypes.float8_e5m2, 14)}[fmt]
    v = np.moveaxis(np.asarray(x, np.float32).astype(ml_dtypes.bfloat16).astype(np.float64), axis, -1)
    blocks = v.reshape(v.shape[:-1] + (-1, 32))
    amax = np.abs(blocks).max(-1, keepdims=True)
    byte = np.maximum(np.where(amax > 0, np.frexp(amax)[1] - 1 + 127, 0) - down, 1)
    scale = np.exp2(byte - 127.0)
    codes = (blocks / scale).astype(np.float32).astype(dtype).astype(np.float64)
    return np.moveaxis((codes * scale).reshape(v.shape), -1, axis)


WIDE = False


def mx_kscale(k):
    if not WIDE:
        return np.ones(k)
    levels = np.array([10, -10, 5, -5, 0])
    if k % 512:
        return np.exp2(np.random.permutation(np.resize(levels, k // 32))).repeat(32)
    a = np.empty((k // 512, 16))
    for p in range(k // 512):
        a[p, :8] = np.random.permutation(np.resize(levels, 8))
        for g in range(8):
            far = levels[np.abs(levels - a[p, g]) >= 10]
            a[p, g + 8] = far[np.random.randint(len(far))]
    return np.exp2(a.ravel()).repeat(32)


def f64(x):
    return np.asarray(x).astype(np.float64)


def striped8(idx):
    return np.asarray(idx).reshape(8, -1, 16).transpose(0, 2, 1).reshape(128, -1).astype(np.uint16)


def unstriped8(offs):
    return offs.reshape(8, 16, -1).transpose(0, 2, 1).reshape(8, -1).astype(np.int64)


def pick8(x, idx, run):
    r = np.arange(len(x))
    return x[r[:, None], idx[r % (8 * run) // run]]


E2M1 = np.array([0.0, 0.5, 1.0, 1.5, 2.0, 3.0, 4.0, 6.0, -0.0, -0.5, -1.0, -1.5, -2.0, -3.0, -4.0, -6.0])


def pack_weight(w, fmt):
    k, n = w.shape
    w = f64(np.asarray(w, np.float32).astype(ml_dtypes.bfloat16)).reshape(k // 32, 32, n)
    amax = np.abs(w).max(1)
    if fmt == "e4m3":
        byte = np.frexp(amax)[1] - 1 + 127 - 7
    else:
        mant, ex = np.frexp(amax / 6.0)
        byte = np.where(mant > 0.5, ex, ex - 1) + 127
    byte = np.clip(np.where(amax > 0, byte, 1), 1, 254)
    scaled = (w * np.exp2(127.0 - byte)[:, None, :]).reshape(k, n).astype(np.float32)
    by_word = np.ascontiguousarray(scaled.reshape(k // 512, 128, 4, n).transpose(0, 1, 3, 2))
    if fmt == "e4m3":
        words = by_word.astype(ml_dtypes.float8_e4m3fn).view(np.uint8)
    else:
        c = by_word.astype(ml_dtypes.float4_e2m1fn).view(np.uint8) & 0xF
        words = (c[..., 0::2] | (c[..., 1::2] << 4)).reshape(k // 512, 128, 2 * n)
    return np.ascontiguousarray(words), np.ascontiguousarray(byte.astype(np.uint8).reshape(k // 512, 16, n))


def unpack_weight(words, scales, fmt):
    g, _, n = scales.shape
    words = np.ascontiguousarray(words).reshape(g, 128, n, -1)
    if fmt == "e4m3":
        vals = words.view(ml_dtypes.float8_e4m3fn).astype(np.float64)
    else:
        nib = np.empty((g, 128, n, 4), np.uint8)
        nib[..., 0::2] = words & 0xF
        nib[..., 1::2] = words >> 4
        vals = E2M1[nib]
    vals = vals * np.repeat(np.exp2(scales.astype(np.float64) - 127.0), 8, axis=1)[..., None]
    return vals.transpose(0, 1, 3, 2).reshape(g * 512, n)


D, V, Q, I = 512, 2048, 128, 512


def setup_inputs():
    n = np.random.standard_normal
    idx = np.stack([np.random.permutation(V)[:I] for _ in range(8)])
    idx2 = np.stack([np.random.permutation(V)[:I] for _ in range(8)])
    fd = mx_kscale(D)
    vocp = pack_weight(n((D, V)) / fd[:, None], "e2m1")
    return {
        "hid": (n((D, Q)) * 0.8 / np.sqrt(D) * fd[:, None]).astype(np.float32),
        "voc_words": vocp[0],
        "voc_scales": vocp[1],
        "target": (np.random.uniform(0.0, 2.0, (Q, I))).astype(np.float32),
        "old": (0.5 * n((Q, V))).astype(np.float32),
        "offs": striped8(idx),
        "offs2": striped8(idx2),
    }


def reference(hid, voc_words, voc_scales, target, old, offs, offs2):
    idx = unstriped8(offs)
    idx2 = unstriped8(offs2)
    vocu = unpack_weight(voc_words, voc_scales, "e2m1")
    hidq = mxq(f64(hid), 0, "e4m3")
    a = hidq.T @ vocu
    p = np.exp(pick8(a, idx, 16))
    z = np.sum(p, axis=1, keepdims=True)
    b = np.exp(pick8(a, idx2, 16)) / z * 512.0
    db = f64(target) / (b + 1.0)
    dz = np.sum(db * 512.0 * np.exp(pick8(a, idx2, 16)) / np.square(z) * (-1.0), axis=1, keepdims=True)
    e1 = db * 512.0 / z * np.exp(pick8(a, idx2, 16))
    s1 = np.zeros((Q, V))
    s1[np.arange(Q)[:, None], idx2[np.arange(Q) % 128 // 16]] = e1
    e2 = dz * p
    s2 = np.zeros((Q, V))
    s2[np.arange(Q)[:, None], idx[np.arange(Q) % 128 // 16]] = e2
    da = s1 + s2
    y = da + f64(old)
    return y

@@ -1,0 +1,166 @@
+import math
+from contextlib import ExitStack
+
+import concourse.mybir as mybir
+
+D, V, Q, I = 512, 2048, 128, 512
+FLOPS = 2 * D * Q * V
+
+F32 = mybir.dt.float32
+BF16 = mybir.dt.bfloat16
+I32 = mybir.dt.int32
+U32 = mybir.dt.uint32
+U16 = mybir.dt.uint16
+U8 = mybir.dt.uint8
+FP8X4 = mybir.dt.float8_e4m3fn_x4
+FP4X4 = mybir.dt.float4_e2m1fn_x4
+ALU = mybir.AluOpType
+ACT = mybir.ActivationFunctionType
+
+P = 128
+PACK = 4
+N_MM = 256
+WORD_TILES = 2
+OUT_WIDTHS = (256, 512, 512, 512, 256)
+
+LN2 = math.log(2.0)
+BITS_SLOPE = LN2 / 2.0**23
+BITS_SHIFT = (127.0 - 0.043) * LN2
+
+
+def tile_attend_ballowed_heads_kernel(tc, hid, voc_words, voc_scales, target, old, offs, offs2, out):
+    nc = tc.nc
+    with ExitStack() as ctx:
+        keep = ctx.enter_context(tc.tile_pool(name="keep", bufs=1))
+        psum = ctx.enter_context(tc.psum_pool(name="psum", bufs=1))
+
+        def column(name):
+            return keep.tile([P, 1], F32, name=name)
+
+        list1 = keep.tile([P, I // 16], U16, name="list1")
+        list2 = keep.tile([P, I // 16], U16, name="list2")
+        hid_raw = keep.tile([P, PACK, Q], F32, name="hid_raw")
+        voc_plane = keep.tile([P, V], U8, name="voc_plane", align_bytes=64)
+        span = V // WORD_TILES
+        words = [keep.tile([P, 2 * span], U8, name="words%d" % w, align_bytes=64) for w in range(WORD_TILES)]
+        tgt = keep.tile([P, I], F32, name="tgt")
+        before = keep.tile([P, V], F32, name="before")
+        placed2 = keep.tile([P, V], F32, name="placed2")
+
+        nc.gpsimd.memset(voc_plane[:].bitcast(I32), 0)
+        nc.sync.dma_start(out=hid_raw[:], in_=hid.rearrange("(p j) q -> p j q", j=PACK))
+        for quad in range(4):
+            nc.sync.dma_start(
+                out=voc_plane[32 * quad : 32 * quad + 4, :].bitcast(I32),
+                in_=voc_scales[0, 4 * quad : 4 * quad + 4, :].bitcast(I32),
+            )
+        for w in range(WORD_TILES):
+            nc.sync.dma_start(
+                out=words[w][:].bitcast(I32),
+                in_=voc_words[0, :, 2 * span * w : 2 * span * (w + 1)].bitcast(I32),
+            )
+        nc.sync.dma_start(list1[:], offs)
+        nc.sync.dma_start(list2[:], offs2)
+        nc.sync.dma_start(out=tgt[:], in_=target)
+        nc.sync.dma_start(out=before[:], in_=old)
+        nc.vector.memset(placed2[:], 0.0)
+
+        grouped = keep.tile([P, Q, PACK], BF16, name="grouped", tag="reused", align_bytes=64)
+        hid_codes = keep.tile([P, Q], U32, name="hid_codes", align_bytes=64)
+        hid_plane = keep.tile([P, Q], U8, name="hid_plane", align_bytes=64)
+        nc.vector.tensor_copy(out=grouped[:], in_=hid_raw[:].rearrange("p j q -> p q j"))
+        nc.vector.quantize_mx(
+            out=hid_codes[:].bitcast(FP8X4),
+            scales=hid_plane[:],
+            in_=grouped[:].rearrange("p q j -> p (q j)"),
+        )
+
+        placed1 = keep.tile([P, V], F32, name="placed1", tag="reused", align_bytes=64)
+        nc.gpsimd.memset(placed1[:], 0.0)
+
+        scores = keep.tile([P, V], F32, name="scores")
+        for n in range(V // N_MM):
+            cols = slice(n * N_MM, (n + 1) * N_MM)
+            w, first = divmod(n * N_MM, span)
+            bank = psum.tile([P, N_MM], F32, name="bank%d" % n)
+            nc.tensor.matmul_mx(
+                out=bank[:],
+                lhsT=hid_codes[:].bitcast(FP8X4),
+                lhsT_scale=hid_plane[:],
+                rhs=words[w][:, 2 * first : 2 * (first + N_MM)].bitcast(FP4X4),
+                rhs_scale=voc_plane[:, cols],
+                start=True,
+                stop=True,
+            )
+            if n % 2 == 0:
+                nc.scalar.copy(out=scores[:, cols], in_=bank[:])
+            else:
+                nc.vector.tensor_copy(out=scores[:, cols], in_=bank[:])
+
+        half_tgt = keep.tile([P, I], F32, name="half_tgt")
+        nc.gpsimd.tensor_scalar(half_tgt[:], tgt[:], -0.5, 0.0, ALU.mult, ALU.add)
+
+        picked = keep.tile([P, I], F32, name="picked")
+        negated = keep.tile([P, I], F32, name="negated")
+        neg_max = column("neg_max")
+        nc.vector.tensor_copy(picked[:], scores[:].indirect(list1[:]))
+        nc.vector.tensor_scalar(negated[:], picked[:], -1.0, None, ALU.mult, ALU.min, accum_out=neg_max[:])
+        nc.vector.tensor_copy(picked[:], scores[:].indirect(list2[:]))
+
+        p = keep.tile([P, I], F32, name="p")
+        z = column("z")
+        nc.scalar.activation(p[:], negated[:], ACT.Exp, bias=neg_max[:], scale=-1.0, accum_out=z[:])
+        nc.vector.tensor_copy(placed2[:].indirect(list1[:]), p[:])
+
+        shift = column("shift")
+        exp0 = column("exp0")
+        start0 = column("start0")
+        square0 = column("square0")
+        z_small = column("z_small")
+        base0 = column("base0")
+        exp1 = column("exp1")
+        base1 = column("base1")
+        square1 = column("square1")
+        bias = column("bias")
+        z_bits = z[:].bitcast(U32)
+        nc.scalar.activation(shift[:], neg_max[:], ACT.Identity, bias=0.25, scale=-0.5)
+        nc.scalar.activation(exp0[:], z_bits, ACT.Exp, bias=BITS_SHIFT, scale=-BITS_SLOPE)
+        nc.scalar.activation(start0[:], z_bits, ACT.Identity, bias=BITS_SHIFT - 0.5 + 9.0 * LN2, scale=-BITS_SLOPE)
+        nc.scalar.activation(square0[:], exp0[:], ACT.Square, bias=-2.0, scale=z[:])
+        nc.scalar.activation(z_small[:], z[:], ACT.Copy, scale=1.0 / 512.0)
+        nc.scalar.activation(base0[:], start0[:], ACT.Identity, bias=shift[:], scale=-0.5)
+        nc.scalar.activation(exp1[:], square0[:], ACT.Exp, bias=start0[:], scale=0.5)
+        nc.scalar.activation(base1[:], square0[:], ACT.Identity, bias=base0[:], scale=-0.25)
+        nc.scalar.activation(square1[:], exp1[:], ACT.Square, bias=-2.0, scale=z_small[:])
+        nc.scalar.activation(bias[:], square1[:], ACT.Identity, bias=base1[:], scale=-0.25)
+        th = keep.tile([P, I], F32, name="th")
+        nc.scalar.activation(th[:], picked[:], ACT.Tanh, bias=bias[:], scale=-0.5)
+        row_max = column("row_max")
+        inv_small = column("inv_small")
+        neg_inv_z = column("neg_inv_z")
+        nc.scalar.activation(row_max[:], neg_max[:], ACT.Copy, scale=-1.0)
+        nc.scalar.activation(inv_small[:], bias[:], ACT.Exp, bias=row_max[:], scale=-2.0)
+        nc.scalar.activation(neg_inv_z[:], inv_small[:], ACT.Copy, scale=-1.0 / 512.0)
+
+        e1 = keep.tile([P, I], F32, name="e1")
+        total = column("total")
+        nc.vector.scalar_tensor_tensor(e1[:], th[:], -1.0, half_tgt[:], ALU.add, ALU.mult, accum_out=total[:])
+        nc.vector.tensor_copy(placed1[:].indirect(list2[:]), e1[:])
+        factor = column("factor")
+        nc.scalar.activation(factor[:], total[:], ACT.Copy, scale=neg_inv_z[:])
+
+        starts = [sum(OUT_WIDTHS[:b]) for b in range(len(OUT_WIDTHS))]
+        partials = []
+        for b in range(len(OUT_WIDTHS) + 1):
+            if b < len(OUT_WIDTHS):
+                cols = slice(starts[b], starts[b] + OUT_WIDTHS[b])
+                partial = keep.tile([P, OUT_WIDTHS[b]], F32, name="partial%d" % b)
+                nc.vector.scalar_tensor_tensor(
+                    partial[:], placed2[:, cols], factor[:], before[:, cols], ALU.mult, ALU.add
+                )
+                partials.append(partial)
+            if b > 0:
+                cols = slice(starts[b - 1], starts[b - 1] + OUT_WIDTHS[b - 1])
+                result = keep.tile([P, OUT_WIDTHS[b - 1]], F32, name="result%d" % b)
+                nc.vector.tensor_tensor(result[:], partials[b - 1][:], placed1[:, cols], ALU.add)
+                nc.sync.dma_start(out=out[:, cols], in_=result[:])

@@ -19,9 +19,11 @@ ACT = mybir.ActivationFunctionType
 
 P = 128
 PACK = 4
-N_MM = 256
-WORD_TILES = 2
-OUT_WIDTHS = (256, 512, 512, 512, 256)
+MM_WIDTHS = (512, 512, 256, 256, 256, 128, 128)
+SCALAR_BANKS = (0, 2, 4)
+WORD_SPANS = (512, 1536)
+SIDE_WIDTHS = (192, 352, 352)
+REST_WIDTH = 288
 
 LN2 = math.log(2.0)
 BITS_SLOPE = LN2 / 2.0**23
@@ -39,12 +41,10 @@ def tile_attend_ballowed_heads_kernel(tc, hid, voc_words, voc_scales, target, ol
 
         list1 = keep.tile([P, I // 16], U16, name="list1")
         list2 = keep.tile([P, I // 16], U16, name="list2")
-        hid_raw = keep.tile([P, PACK, Q], F32, name="hid_raw")
+        hid_raw = keep.tile([P, PACK, Q], F32, name="hid_raw", tag="raw_then_target")
         voc_plane = keep.tile([P, V], U8, name="voc_plane", align_bytes=64)
-        span = V // WORD_TILES
-        words = [keep.tile([P, 2 * span], U8, name="words%d" % w, align_bytes=64) for w in range(WORD_TILES)]
-        tgt = keep.tile([P, I], F32, name="tgt")
-        before = keep.tile([P, V], F32, name="before")
+        words = [keep.tile([P, 2 * span], U8, name="words%d" % w, align_bytes=64) for w, span in enumerate(WORD_SPANS)]
+        word_starts = [sum(WORD_SPANS[:w]) for w in range(len(WORD_SPANS))]
         placed2 = keep.tile([P, V], F32, name="placed2")
 
         nc.gpsimd.memset(voc_plane[:].bitcast(I32), 0)
@@ -54,19 +54,21 @@ def tile_attend_ballowed_heads_kernel(tc, hid, voc_words, voc_scales, target, ol
                 out=voc_plane[32 * quad : 32 * quad + 4, :].bitcast(I32),
                 in_=voc_scales[0, 4 * quad : 4 * quad + 4, :].bitcast(I32),
             )
-        for w in range(WORD_TILES):
+        for w, span in enumerate(WORD_SPANS):
             nc.sync.dma_start(
                 out=words[w][:].bitcast(I32),
-                in_=voc_words[0, :, 2 * span * w : 2 * span * (w + 1)].bitcast(I32),
+                in_=voc_words[0, :, 2 * word_starts[w] : 2 * (word_starts[w] + span)].bitcast(I32),
             )
         nc.sync.dma_start(list1[:], offs)
         nc.sync.dma_start(list2[:], offs2)
-        nc.sync.dma_start(out=tgt[:], in_=target)
-        nc.sync.dma_start(out=before[:], in_=old)
+        one = column("one")
+        offset = column("offset")
+        nc.vector.memset(one[:], 1.0)
+        nc.scalar.activation(offset[:], one[:], ACT.Copy, scale=0.25 - 0.5 * math.log(512.0))
         nc.vector.memset(placed2[:], 0.0)
 
         grouped = keep.tile([P, Q, PACK], BF16, name="grouped", tag="reused", align_bytes=64)
-        hid_codes = keep.tile([P, Q], U32, name="hid_codes", align_bytes=64)
+        hid_codes = keep.tile([P, Q], U32, name="hid_codes", tag="codes_then_old", align_bytes=64)
         hid_plane = keep.tile([P, Q], U8, name="hid_plane", align_bytes=64)
         nc.vector.tensor_copy(out=grouped[:], in_=hid_raw[:].rearrange("p j q -> p q j"))
         nc.vector.quantize_mx(
@@ -75,28 +77,34 @@ def tile_attend_ballowed_heads_kernel(tc, hid, voc_words, voc_scales, target, ol
             in_=grouped[:].rearrange("p q j -> p (q j)"),
         )
 
+        tgt = keep.tile([P, I], F32, name="tgt", tag="raw_then_target")
+        nc.sync.dma_start(out=tgt[:], in_=target)
         placed1 = keep.tile([P, V], F32, name="placed1", tag="reused", align_bytes=64)
         nc.gpsimd.memset(placed1[:], 0.0)
 
         scores = keep.tile([P, V], F32, name="scores")
-        for n in range(V // N_MM):
-            cols = slice(n * N_MM, (n + 1) * N_MM)
-            w, first = divmod(n * N_MM, span)
-            bank = psum.tile([P, N_MM], F32, name="bank%d" % n)
+        for n, width in enumerate(MM_WIDTHS):
+            col = sum(MM_WIDTHS[:n])
+            cols = slice(col, col + width)
+            w = max(k for k, start in enumerate(word_starts) if start <= col)
+            first = col - word_starts[w]
+            bank = psum.tile([P, width], F32, name="bank%d" % n)
             nc.tensor.matmul_mx(
                 out=bank[:],
                 lhsT=hid_codes[:].bitcast(FP8X4),
                 lhsT_scale=hid_plane[:],
-                rhs=words[w][:, 2 * first : 2 * (first + N_MM)].bitcast(FP4X4),
+                rhs=words[w][:, 2 * first : 2 * (first + width)].bitcast(FP4X4),
                 rhs_scale=voc_plane[:, cols],
                 start=True,
                 stop=True,
             )
-            if n % 2 == 0:
+            if n in SCALAR_BANKS:
                 nc.scalar.copy(out=scores[:, cols], in_=bank[:])
             else:
                 nc.vector.tensor_copy(out=scores[:, cols], in_=bank[:])
 
+        before = keep.tile([P, V], F32, name="before", tag="codes_then_old", align_bytes=64)
+        nc.sync.dma_start(out=before[:], in_=old)
         half_tgt = keep.tile([P, I], F32, name="half_tgt")
         nc.gpsimd.tensor_scalar(half_tgt[:], tgt[:], -0.5, 0.0, ALU.mult, ALU.add)
 
@@ -116,22 +124,20 @@ def tile_attend_ballowed_heads_kernel(tc, hid, voc_words, voc_scales, target, ol
         exp0 = column("exp0")
         start0 = column("start0")
         square0 = column("square0")
-        z_small = column("z_small")
         base0 = column("base0")
         exp1 = column("exp1")
         base1 = column("base1")
-        square1 = column("square1")
         bias = column("bias")
         z_bits = z[:].bitcast(U32)
-        nc.scalar.activation(shift[:], neg_max[:], ACT.Identity, bias=0.25, scale=-0.5)
+        nc.scalar.activation(shift[:], neg_max[:], ACT.Identity, bias=offset[:], scale=-0.5)
         nc.scalar.activation(exp0[:], z_bits, ACT.Exp, bias=BITS_SHIFT, scale=-BITS_SLOPE)
-        nc.scalar.activation(start0[:], z_bits, ACT.Identity, bias=BITS_SHIFT - 0.5 + 9.0 * LN2, scale=-BITS_SLOPE)
+        nc.scalar.activation(start0[:], z_bits, ACT.Identity, bias=BITS_SHIFT - 0.5, scale=-BITS_SLOPE)
         nc.scalar.activation(square0[:], exp0[:], ACT.Square, bias=-2.0, scale=z[:])
-        nc.scalar.activation(z_small[:], z[:], ACT.Copy, scale=1.0 / 512.0)
         nc.scalar.activation(base0[:], start0[:], ACT.Identity, bias=shift[:], scale=-0.5)
         nc.scalar.activation(exp1[:], square0[:], ACT.Exp, bias=start0[:], scale=0.5)
         nc.scalar.activation(base1[:], square0[:], ACT.Identity, bias=base0[:], scale=-0.25)
-        nc.scalar.activation(square1[:], exp1[:], ACT.Square, bias=-2.0, scale=z_small[:])
+        square1 = column("square1")
+        nc.scalar.activation(square1[:], exp1[:], ACT.Square, bias=-2.0, scale=z[:])
         nc.scalar.activation(bias[:], square1[:], ACT.Identity, bias=base1[:], scale=-0.25)
         th = keep.tile([P, I], F32, name="th")
         nc.scalar.activation(th[:], picked[:], ACT.Tanh, bias=bias[:], scale=-0.5)
@@ -149,18 +155,34 @@ def tile_attend_ballowed_heads_kernel(tc, hid, voc_words, voc_scales, target, ol
         factor = column("factor")
         nc.scalar.activation(factor[:], total[:], ACT.Copy, scale=neg_inv_z[:])
 
-        starts = [sum(OUT_WIDTHS[:b]) for b in range(len(OUT_WIDTHS))]
-        partials = []
-        for b in range(len(OUT_WIDTHS) + 1):
-            if b < len(OUT_WIDTHS):
-                cols = slice(starts[b], starts[b] + OUT_WIDTHS[b])
-                partial = keep.tile([P, OUT_WIDTHS[b]], F32, name="partial%d" % b)
+        def finish(first, width, partial):
+            cols = slice(first, first + width)
+            result = keep.tile([P, width], F32, name="result%d" % first)
+            nc.vector.tensor_tensor(result[:], partial, placed1[:, cols], ALU.add)
+            nc.sync.dma_start(out=out[:, cols], in_=result[:])
+
+        first = 0
+        for b, width in enumerate(SIDE_WIDTHS):
+            cols = slice(first, first + width)
+            scaled = keep.tile([P, width], F32, name="scaled%d" % b, tag="scaled%d" % b)
+            partial = keep.tile([P, width], F32, name="partial%d" % b)
+            nc.scalar.activation(scaled[:], placed2[:, cols], ACT.Copy, scale=factor[:])
+            nc.gpsimd.tensor_tensor(partial[:], scaled[:], before[:, cols], ALU.add)
+            finish(first, width, partial[:])
+            first += width
+
+        rest = keep.tile([P, V - first], F32, name="rest", tag="scaled%d" % (len(SIDE_WIDTHS) - 1))
+        pieces = (V - first) // REST_WIDTH
+        for k in range(pieces + 1):
+            if k < pieces:
+                cols = slice(first + k * REST_WIDTH, first + (k + 1) * REST_WIDTH)
                 nc.vector.scalar_tensor_tensor(
-                    partial[:], placed2[:, cols], factor[:], before[:, cols], ALU.mult, ALU.add
+                    rest[:, k * REST_WIDTH : (k + 1) * REST_WIDTH],
+                    placed2[:, cols],
+                    factor[:],
+                    before[:, cols],
+                    ALU.mult,
+                    ALU.add,
                 )
-                partials.append(partial)
-            if b > 0:
-                cols = slice(starts[b - 1], starts[b - 1] + OUT_WIDTHS[b - 1])
-                result = keep.tile([P, OUT_WIDTHS[b - 1]], F32, name="result%d" % b)
-                nc.vector.tensor_tensor(result[:], partials[b - 1][:], placed1[:, cols], ALU.add)
-                nc.sync.dma_start(out=out[:, cols], in_=result[:])
+            if k > 0:
+                finish(first + (k - 1) * REST_WIDTH, REST_WIDTH, rest[:, (k - 1) * REST_WIDTH : k * REST_WIDTH])

@@ -2,6 +2,7 @@ import math
 from contextlib import ExitStack
 
 import concourse.mybir as mybir
+from concourse.masks import make_identity
 
 D, V, Q, I = 512, 2048, 128, 512
 FLOPS = 2 * D * Q * V
@@ -22,8 +23,10 @@ PACK = 4
 MM_WIDTHS = (512, 512, 256, 256, 256, 128, 128)
 SCALAR_BANKS = (0, 2, 4)
 WORD_SPANS = (512, 1536)
-SIDE_WIDTHS = (192, 352, 352)
-REST_WIDTH = 288
+SIDE_WIDTHS = (256, 384, 384)
+TURN_WIDTH = 512
+TURN_BLOCKS = 2
+TURN_STORES = ((512,), (320, 192))
 
 LN2 = math.log(2.0)
 BITS_SLOPE = LN2 / 2.0**23
@@ -88,7 +91,7 @@ def tile_attend_ballowed_heads_kernel(tc, hid, voc_words, voc_scales, target, ol
             cols = slice(col, col + width)
             w = max(k for k, start in enumerate(word_starts) if start <= col)
             first = col - word_starts[w]
-            bank = psum.tile([P, width], F32, name="bank%d" % n)
+            bank = psum.tile([P, width], F32, name="bank%d" % n, tag="bank%d" % n)
             nc.tensor.matmul_mx(
                 out=bank[:],
                 lhsT=hid_codes[:].bitcast(FP8X4),
@@ -105,6 +108,23 @@ def tile_attend_ballowed_heads_kernel(tc, hid, voc_words, voc_scales, target, ol
 
         before = keep.tile([P, V], F32, name="before", tag="codes_then_old", align_bytes=64)
         nc.sync.dma_start(out=before[:], in_=old)
+        identity = keep.tile([P, P], F32, name="identity")
+        make_identity(nc, identity[:])
+        turn_first = sum(SIDE_WIDTHS)
+        turned = []
+        for r in range(TURN_BLOCKS):
+            bank = psum.tile([P, TURN_WIDTH], F32, name="turned%d" % r, tag="bank%d" % r)
+            for j in range(TURN_WIDTH // P):
+                col = turn_first + r * TURN_WIDTH + j * P
+                nc.tensor.matmul(
+                    bank[:, j * P : (j + 1) * P],
+                    before[:, col : col + P],
+                    identity[:],
+                    start=(j == 0),
+                    stop=False,
+                    is_transpose=True,
+                )
+            turned.append(bank)
         half_tgt = keep.tile([P, I], F32, name="half_tgt")
         nc.gpsimd.tensor_scalar(half_tgt[:], tgt[:], -0.5, 0.0, ALU.mult, ALU.add)
 
@@ -161,28 +181,40 @@ def tile_attend_ballowed_heads_kernel(tc, hid, voc_words, voc_scales, target, ol
             nc.vector.tensor_tensor(result[:], partial, placed1[:, cols], ALU.add)
             nc.sync.dma_start(out=out[:, cols], in_=result[:])
 
-        first = 0
-        for b, width in enumerate(SIDE_WIDTHS):
-            cols = slice(first, first + width)
-            scaled = keep.tile([P, width], F32, name="scaled%d" % b, tag="scaled%d" % b)
-            partial = keep.tile([P, width], F32, name="partial%d" % b)
-            nc.scalar.activation(scaled[:], placed2[:, cols], ACT.Copy, scale=factor[:])
-            nc.gpsimd.tensor_tensor(partial[:], scaled[:], before[:, cols], ALU.add)
-            finish(first, width, partial[:])
-            first += width
+        def scale(first, width):
+            scaled = keep.tile([P, width], F32, name="scaled%d" % first)
+            nc.scalar.activation(scaled[:], placed2[:, first : first + width], ACT.Copy, scale=factor[:])
+            return scaled
 
-        rest = keep.tile([P, V - first], F32, name="rest", tag="scaled%d" % (len(SIDE_WIDTHS) - 1))
-        pieces = (V - first) // REST_WIDTH
-        for k in range(pieces + 1):
-            if k < pieces:
-                cols = slice(first + k * REST_WIDTH, first + (k + 1) * REST_WIDTH)
-                nc.vector.scalar_tensor_tensor(
-                    rest[:, k * REST_WIDTH : (k + 1) * REST_WIDTH],
-                    placed2[:, cols],
-                    factor[:],
-                    before[:, cols],
-                    ALU.mult,
-                    ALU.add,
-                )
-            if k > 0:
-                finish(first + (k - 1) * REST_WIDTH, REST_WIDTH, rest[:, (k - 1) * REST_WIDTH : k * REST_WIDTH])
+        partials = []
+        for b, width in enumerate(SIDE_WIDTHS):
+            first = sum(SIDE_WIDTHS[:b])
+            scaled = scale(first, width)
+            partial = keep.tile([P, width], F32, name="partial%d" % b)
+            nc.gpsimd.tensor_tensor(partial[:], scaled[:], before[:, first : first + width], ALU.add)
+            partials.append(partial)
+            if b < TURN_BLOCKS:
+                scaled = scale(turn_first + b * TURN_WIDTH, TURN_WIDTH)
+                for j in range(TURN_WIDTH // P):
+                    nc.tensor.matmul(
+                        turned[b][:, j * P : (j + 1) * P],
+                        scaled[:, j * P : (j + 1) * P],
+                        identity[:],
+                        start=False,
+                        stop=(j == TURN_WIDTH // P - 1),
+                        is_transpose=True,
+                    )
+        back = []
+        for r in range(TURN_BLOCKS):
+            summed = keep.tile([P, TURN_WIDTH], F32, name="summed%d" % r)
+            nc.scalar.copy(out=summed[:], in_=turned[r][:])
+            bank = psum.tile([P, TURN_WIDTH], F32, name="back%d" % r, tag="bank%d" % (TURN_BLOCKS + r))
+            for j in range(TURN_WIDTH // P):
+                nc.tensor.transpose(bank[:, j * P : (j + 1) * P], summed[:, j * P : (j + 1) * P], identity[:])
+            back.append(bank)
+        for b, width in enumerate(SIDE_WIDTHS):
+            finish(sum(SIDE_WIDTHS[:b]), width, partials[b][:])
+        for r in range(TURN_BLOCKS):
+            for k, width in enumerate(TURN_STORES[r]):
+                first = sum(TURN_STORES[r][:k])
+                finish(turn_first + r * TURN_WIDTH + first, width, back[r][:, first : first + width])

@@ -22,11 +22,10 @@ P = 128
 PACK = 4
 MM_WIDTHS = (512, 512, 256, 256, 256, 128, 128)
 SCALAR_BANKS = (0, 2, 4)
-WORD_SPANS = (512, 1536)
-SIDE_WIDTHS = (256, 384, 384)
-TURN_WIDTH = 512
-TURN_BLOCKS = 2
-TURN_STORES = ((512,), (320, 192))
+WORD_SPANS = (512, 512, 1024)
+SIDE_WIDTHS = (320, 576)
+TURN_WIDTHS = (512, 384, 256)
+TURN_LAG = 2
 
 LN2 = math.log(2.0)
 BITS_SLOPE = LN2 / 2.0**23
@@ -110,12 +109,12 @@ def tile_attend_ballowed_heads_kernel(tc, hid, voc_words, voc_scales, target, ol
         nc.sync.dma_start(out=before[:], in_=old)
         identity = keep.tile([P, P], F32, name="identity")
         make_identity(nc, identity[:])
-        turn_first = sum(SIDE_WIDTHS)
+        turn_starts = [sum(SIDE_WIDTHS) + sum(TURN_WIDTHS[:r]) for r in range(len(TURN_WIDTHS))]
         turned = []
-        for r in range(TURN_BLOCKS):
-            bank = psum.tile([P, TURN_WIDTH], F32, name="turned%d" % r, tag="bank%d" % r)
-            for j in range(TURN_WIDTH // P):
-                col = turn_first + r * TURN_WIDTH + j * P
+        for r, width in enumerate(TURN_WIDTHS):
+            bank = psum.tile([P, width], F32, name="turned%d" % r, tag="bank%d" % r)
+            for j in range(width // P):
+                col = turn_starts[r] + j * P
                 nc.tensor.matmul(
                     bank[:, j * P : (j + 1) * P],
                     before[:, col : col + P],
@@ -125,8 +124,6 @@ def tile_attend_ballowed_heads_kernel(tc, hid, voc_words, voc_scales, target, ol
                     is_transpose=True,
                 )
             turned.append(bank)
-        half_tgt = keep.tile([P, I], F32, name="half_tgt")
-        nc.gpsimd.tensor_scalar(half_tgt[:], tgt[:], -0.5, 0.0, ALU.mult, ALU.add)
 
         picked = keep.tile([P, I], F32, name="picked")
         negated = keep.tile([P, I], F32, name="negated")
@@ -159,26 +156,30 @@ def tile_attend_ballowed_heads_kernel(tc, hid, voc_words, voc_scales, target, ol
         square1 = column("square1")
         nc.scalar.activation(square1[:], exp1[:], ACT.Square, bias=-2.0, scale=z[:])
         nc.scalar.activation(bias[:], square1[:], ACT.Identity, bias=base1[:], scale=-0.25)
-        th = keep.tile([P, I], F32, name="th")
-        nc.scalar.activation(th[:], picked[:], ACT.Tanh, bias=bias[:], scale=-0.5)
         row_max = column("row_max")
+        neg_z = column("neg_z")
         inv_small = column("inv_small")
-        neg_inv_z = column("neg_inv_z")
+        slope = column("slope")
+        level = column("level")
+        th = keep.tile([P, I], F32, name="th")
+        share = keep.tile([P, I], F32, name="share")
         nc.scalar.activation(row_max[:], neg_max[:], ACT.Copy, scale=-1.0)
         nc.scalar.activation(inv_small[:], bias[:], ACT.Exp, bias=row_max[:], scale=-2.0)
-        nc.scalar.activation(neg_inv_z[:], inv_small[:], ACT.Copy, scale=-1.0 / 512.0)
+        nc.scalar.activation(th[:], picked[:], ACT.Tanh, bias=bias[:], scale=-0.5)
+        nc.scalar.activation(slope[:], inv_small[:], ACT.Copy, scale=1.0 / 1024.0)
+        nc.scalar.activation(level[:], inv_small[:], ACT.Copy, scale=-1.0 / 1024.0)
+        nc.scalar.activation(share[:], th[:], ACT.Identity, bias=level[:], scale=slope[:])
+        nc.scalar.activation(neg_z[:], z[:], ACT.Copy, scale=-1.0)
 
         e1 = keep.tile([P, I], F32, name="e1")
-        total = column("total")
-        nc.vector.scalar_tensor_tensor(e1[:], th[:], -1.0, half_tgt[:], ALU.add, ALU.mult, accum_out=total[:])
-        nc.vector.tensor_copy(placed1[:].indirect(list2[:]), e1[:])
         factor = column("factor")
-        nc.scalar.activation(factor[:], total[:], ACT.Copy, scale=neg_inv_z[:])
+        nc.vector.scalar_tensor_tensor(e1[:], share[:], 1.0, tgt[:], ALU.mult, ALU.mult, accum_out=factor[:])
+        nc.vector.tensor_copy(placed1[:].indirect(list2[:]), e1[:])
 
         def finish(first, width, partial):
             cols = slice(first, first + width)
             result = keep.tile([P, width], F32, name="result%d" % first)
-            nc.vector.tensor_tensor(result[:], partial, placed1[:, cols], ALU.add)
+            nc.vector.scalar_tensor_tensor(result[:], placed1[:, cols], neg_z[:], partial, ALU.mult, ALU.add)
             nc.sync.dma_start(out=out[:, cols], in_=result[:])
 
         def scale(first, width):
@@ -187,34 +188,36 @@ def tile_attend_ballowed_heads_kernel(tc, hid, voc_words, voc_scales, target, ol
             return scaled
 
         partials = []
-        for b, width in enumerate(SIDE_WIDTHS):
-            first = sum(SIDE_WIDTHS[:b])
-            scaled = scale(first, width)
-            partial = keep.tile([P, width], F32, name="partial%d" % b)
-            nc.gpsimd.tensor_tensor(partial[:], scaled[:], before[:, first : first + width], ALU.add)
-            partials.append(partial)
-            if b < TURN_BLOCKS:
-                scaled = scale(turn_first + b * TURN_WIDTH, TURN_WIDTH)
-                for j in range(TURN_WIDTH // P):
+        back = []
+        for step in range(len(TURN_WIDTHS) + TURN_LAG):
+            if step < len(SIDE_WIDTHS):
+                first, width = sum(SIDE_WIDTHS[:step]), SIDE_WIDTHS[step]
+                scaled = scale(first, width)
+                partial = keep.tile([P, width], F32, name="partial%d" % step)
+                nc.gpsimd.tensor_tensor(partial[:], scaled[:], before[:, first : first + width], ALU.add)
+                partials.append(partial)
+            if step >= TURN_LAG:
+                r = step - TURN_LAG
+                width = TURN_WIDTHS[r]
+                summed = keep.tile([P, width], F32, name="summed%d" % r)
+                nc.scalar.copy(out=summed[:], in_=turned[r][:])
+                bank = psum.tile([P, width], F32, name="back%d" % r, tag="bank%d" % (len(TURN_WIDTHS) + r))
+                for j in range(width // P):
+                    nc.tensor.transpose(bank[:, j * P : (j + 1) * P], summed[:, j * P : (j + 1) * P], identity[:])
+                back.append(bank)
+            if step < len(TURN_WIDTHS):
+                width = TURN_WIDTHS[step]
+                scaled = scale(turn_starts[step], width)
+                for j in range(width // P):
                     nc.tensor.matmul(
-                        turned[b][:, j * P : (j + 1) * P],
+                        turned[step][:, j * P : (j + 1) * P],
                         scaled[:, j * P : (j + 1) * P],
                         identity[:],
                         start=False,
-                        stop=(j == TURN_WIDTH // P - 1),
+                        stop=(j == width // P - 1),
                         is_transpose=True,
                     )
-        back = []
-        for r in range(TURN_BLOCKS):
-            summed = keep.tile([P, TURN_WIDTH], F32, name="summed%d" % r)
-            nc.scalar.copy(out=summed[:], in_=turned[r][:])
-            bank = psum.tile([P, TURN_WIDTH], F32, name="back%d" % r, tag="bank%d" % (TURN_BLOCKS + r))
-            for j in range(TURN_WIDTH // P):
-                nc.tensor.transpose(bank[:, j * P : (j + 1) * P], summed[:, j * P : (j + 1) * P], identity[:])
-            back.append(bank)
         for b, width in enumerate(SIDE_WIDTHS):
             finish(sum(SIDE_WIDTHS[:b]), width, partials[b][:])
-        for r in range(TURN_BLOCKS):
-            for k, width in enumerate(TURN_STORES[r]):
-                first = sum(TURN_STORES[r][:k])
-                finish(turn_first + r * TURN_WIDTH + first, width, back[r][:, first : first + width])
+        for r, width in enumerate(TURN_WIDTHS):
+            finish(turn_starts[r], width, back[r][:])

@@ -49,7 +49,7 @@ def tile_attend_ballowed_heads_kernel(tc, hid, voc_words, voc_scales, target, ol
         word_starts = [sum(WORD_SPANS[:w]) for w in range(len(WORD_SPANS))]
         placed2 = keep.tile([P, V], F32, name="placed2")
 
-        nc.gpsimd.memset(voc_plane[:].bitcast(I32), 0)
+        nc.vector.memset(voc_plane[:].bitcast(I32), 0)
         nc.sync.dma_start(out=hid_raw[:], in_=hid.rearrange("(p j) q -> p j q", j=PACK))
         for quad in range(4):
             nc.sync.dma_start(
@@ -71,7 +71,7 @@ def tile_attend_ballowed_heads_kernel(tc, hid, voc_words, voc_scales, target, ol
 
         grouped = keep.tile([P, Q, PACK], BF16, name="grouped", tag="reused", align_bytes=64)
         hid_codes = keep.tile([P, Q], U32, name="hid_codes", tag="codes_then_old", align_bytes=64)
-        hid_plane = keep.tile([P, Q], U8, name="hid_plane", align_bytes=64)
+        hid_plane = keep.tile([P, Q], U8, name="hid_plane", tag="plane_then_identity", align_bytes=64)
         nc.vector.tensor_copy(out=grouped[:], in_=hid_raw[:].rearrange("p j q -> p q j"))
         nc.vector.quantize_mx(
             out=hid_codes[:].bitcast(FP8X4),
@@ -107,7 +107,7 @@ def tile_attend_ballowed_heads_kernel(tc, hid, voc_words, voc_scales, target, ol
 
         before = keep.tile([P, V], F32, name="before", tag="codes_then_old", align_bytes=64)
         nc.sync.dma_start(out=before[:], in_=old)
-        identity = keep.tile([P, P], F32, name="identity")
+        identity = keep.tile([P, P], F32, name="identity", tag="plane_then_identity", align_bytes=64)
         make_identity(nc, identity[:])
         turn_starts = [sum(SIDE_WIDTHS) + sum(TURN_WIDTHS[:r]) for r in range(len(TURN_WIDTHS))]
         turned = []

import math
from contextlib import ExitStack

import concourse.mybir as mybir
from concourse.masks import make_identity

D, V, Q, I = 512, 2048, 128, 512
FLOPS = 2 * D * Q * V

F32 = mybir.dt.float32
BF16 = mybir.dt.bfloat16
I32 = mybir.dt.int32
U32 = mybir.dt.uint32
U16 = mybir.dt.uint16
U8 = mybir.dt.uint8
FP8X4 = mybir.dt.float8_e4m3fn_x4
FP4X4 = mybir.dt.float4_e2m1fn_x4
ALU = mybir.AluOpType
ACT = mybir.ActivationFunctionType

P = 128
PACK = 4
MM_WIDTHS = (512, 512, 256, 256, 256, 128, 128)
SCALAR_BANKS = (0, 2, 4)
WORD_SPANS = (512, 512, 1024)
SIDE_WIDTHS = (320, 576)
TURN_WIDTHS = (512, 384, 256)
TURN_LAG = 2

LN2 = math.log(2.0)
BITS_SLOPE = LN2 / 2.0**23
BITS_SHIFT = (127.0 - 0.043) * LN2


def tile_attend_ballowed_heads_kernel(tc, hid, voc_words, voc_scales, target, old, offs, offs2, out):
    nc = tc.nc
    with ExitStack() as ctx:
        keep = ctx.enter_context(tc.tile_pool(name="keep", bufs=1))
        psum = ctx.enter_context(tc.psum_pool(name="psum", bufs=1))

        def column(name):
            return keep.tile([P, 1], F32, name=name)

        list1 = keep.tile([P, I // 16], U16, name="list1")
        list2 = keep.tile([P, I // 16], U16, name="list2")
        hid_raw = keep.tile([P, PACK, Q], F32, name="hid_raw", tag="raw_then_target")
        voc_plane = keep.tile([P, V], U8, name="voc_plane", align_bytes=64)
        words = [keep.tile([P, 2 * span], U8, name="words%d" % w, align_bytes=64) for w, span in enumerate(WORD_SPANS)]
        word_starts = [sum(WORD_SPANS[:w]) for w in range(len(WORD_SPANS))]
        placed2 = keep.tile([P, V], F32, name="placed2")

        nc.vector.memset(voc_plane[:].bitcast(I32), 0)
        nc.sync.dma_start(out=hid_raw[:], in_=hid.rearrange("(p j) q -> p j q", j=PACK))
        for quad in range(4):
            nc.sync.dma_start(
                out=voc_plane[32 * quad : 32 * quad + 4, :].bitcast(I32),
                in_=voc_scales[0, 4 * quad : 4 * quad + 4, :].bitcast(I32),
            )
        for w, span in enumerate(WORD_SPANS):
            nc.sync.dma_start(
                out=words[w][:].bitcast(I32),
                in_=voc_words[0, :, 2 * word_starts[w] : 2 * (word_starts[w] + span)].bitcast(I32),
            )
        nc.sync.dma_start(list1[:], offs)
        nc.sync.dma_start(list2[:], offs2)
        one = column("one")
        offset = column("offset")
        nc.vector.memset(one[:], 1.0)
        nc.scalar.activation(offset[:], one[:], ACT.Copy, scale=0.25 - 0.5 * math.log(512.0))
        nc.vector.memset(placed2[:], 0.0)

        grouped = keep.tile([P, Q, PACK], BF16, name="grouped", tag="reused", align_bytes=64)
        hid_codes = keep.tile([P, Q], U32, name="hid_codes", tag="codes_then_old", align_bytes=64)
        hid_plane = keep.tile([P, Q], U8, name="hid_plane", tag="plane_then_identity", align_bytes=64)
        nc.vector.tensor_copy(out=grouped[:], in_=hid_raw[:].rearrange("p j q -> p q j"))
        nc.vector.quantize_mx(
            out=hid_codes[:].bitcast(FP8X4),
            scales=hid_plane[:],
            in_=grouped[:].rearrange("p q j -> p (q j)"),
        )

        tgt = keep.tile([P, I], F32, name="tgt", tag="raw_then_target")
        nc.sync.dma_start(out=tgt[:], in_=target)
        placed1 = keep.tile([P, V], F32, name="placed1", tag="reused", align_bytes=64)
        nc.gpsimd.memset(placed1[:], 0.0)

        scores = keep.tile([P, V], F32, name="scores")
        for n, width in enumerate(MM_WIDTHS):
            col = sum(MM_WIDTHS[:n])
            cols = slice(col, col + width)
            w = max(k for k, start in enumerate(word_starts) if start <= col)
            first = col - word_starts[w]
            bank = psum.tile([P, width], F32, name="bank%d" % n, tag="bank%d" % n)
            nc.tensor.matmul_mx(
                out=bank[:],
                lhsT=hid_codes[:].bitcast(FP8X4),
                lhsT_scale=hid_plane[:],
                rhs=words[w][:, 2 * first : 2 * (first + width)].bitcast(FP4X4),
                rhs_scale=voc_plane[:, cols],
                start=True,
                stop=True,
            )
            if n in SCALAR_BANKS:
                nc.scalar.copy(out=scores[:, cols], in_=bank[:])
            else:
                nc.vector.tensor_copy(out=scores[:, cols], in_=bank[:])

        before = keep.tile([P, V], F32, name="before", tag="codes_then_old", align_bytes=64)
        nc.sync.dma_start(out=before[:], in_=old)
        identity = keep.tile([P, P], F32, name="identity", tag="plane_then_identity", align_bytes=64)
        make_identity(nc, identity[:])
        turn_starts = [sum(SIDE_WIDTHS) + sum(TURN_WIDTHS[:r]) for r in range(len(TURN_WIDTHS))]
        turned = []
        for r, width in enumerate(TURN_WIDTHS):
            bank = psum.tile([P, width], F32, name="turned%d" % r, tag="bank%d" % r)
            for j in range(width // P):
                col = turn_starts[r] + j * P
                nc.tensor.matmul(
                    bank[:, j * P : (j + 1) * P],
                    before[:, col : col + P],
                    identity[:],
                    start=(j == 0),
                    stop=False,
                    is_transpose=True,
                )
            turned.append(bank)

        picked = keep.tile([P, I], F32, name="picked")
        negated = keep.tile([P, I], F32, name="negated")
        neg_max = column("neg_max")
        nc.vector.tensor_copy(picked[:], scores[:].indirect(list1[:]))
        nc.vector.tensor_scalar(negated[:], picked[:], -1.0, None, ALU.mult, ALU.min, accum_out=neg_max[:])
        nc.vector.tensor_copy(picked[:], scores[:].indirect(list2[:]))

        p = keep.tile([P, I], F32, name="p")
        z = column("z")
        nc.scalar.activation(p[:], negated[:], ACT.Exp, bias=neg_max[:], scale=-1.0, accum_out=z[:])
        nc.vector.tensor_copy(placed2[:].indirect(list1[:]), p[:])

        shift = column("shift")
        exp0 = column("exp0")
        start0 = column("start0")
        square0 = column("square0")
        base0 = column("base0")
        exp1 = column("exp1")
        base1 = column("base1")
        bias = column("bias")
        z_bits = z[:].bitcast(U32)
        nc.scalar.activation(shift[:], neg_max[:], ACT.Identity, bias=offset[:], scale=-0.5)
        nc.scalar.activation(exp0[:], z_bits, ACT.Exp, bias=BITS_SHIFT, scale=-BITS_SLOPE)
        nc.scalar.activation(start0[:], z_bits, ACT.Identity, bias=BITS_SHIFT - 0.5, scale=-BITS_SLOPE)
        nc.scalar.activation(square0[:], exp0[:], ACT.Square, bias=-2.0, scale=z[:])
        nc.scalar.activation(base0[:], start0[:], ACT.Identity, bias=shift[:], scale=-0.5)
        nc.scalar.activation(exp1[:], square0[:], ACT.Exp, bias=start0[:], scale=0.5)
        nc.scalar.activation(base1[:], square0[:], ACT.Identity, bias=base0[:], scale=-0.25)
        square1 = column("square1")
        nc.scalar.activation(square1[:], exp1[:], ACT.Square, bias=-2.0, scale=z[:])
        nc.scalar.activation(bias[:], square1[:], ACT.Identity, bias=base1[:], scale=-0.25)
        row_max = column("row_max")
        neg_z = column("neg_z")
        inv_small = column("inv_small")
        slope = column("slope")
        level = column("level")
        th = keep.tile([P, I], F32, name="th")
        share = keep.tile([P, I], F32, name="share")
        nc.scalar.activation(row_max[:], neg_max[:], ACT.Copy, scale=-1.0)
        nc.scalar.activation(inv_small[:], bias[:], ACT.Exp, bias=row_max[:], scale=-2.0)
        nc.scalar.activation(th[:], picked[:], ACT.Tanh, bias=bias[:], scale=-0.5)
        nc.scalar.activation(slope[:], inv_small[:], ACT.Copy, scale=1.0 / 1024.0)
        nc.scalar.activation(level[:], inv_small[:], ACT.Copy, scale=-1.0 / 1024.0)
        nc.scalar.activation(share[:], th[:], ACT.Identity, bias=level[:], scale=slope[:])
        nc.scalar.activation(neg_z[:], z[:], ACT.Copy, scale=-1.0)

        e1 = keep.tile([P, I], F32, name="e1")
        factor = column("factor")
        nc.vector.scalar_tensor_tensor(e1[:], share[:], 1.0, tgt[:], ALU.mult, ALU.mult, accum_out=factor[:])
        nc.vector.tensor_copy(placed1[:].indirect(list2[:]), e1[:])

        def finish(first, width, partial):
            cols = slice(first, first + width)
            result = keep.tile([P, width], F32, name="result%d" % first)
            nc.vector.scalar_tensor_tensor(result[:], placed1[:, cols], neg_z[:], partial, ALU.mult, ALU.add)
            nc.sync.dma_start(out=out[:, cols], in_=result[:])

        def scale(first, width):
            scaled = keep.tile([P, width], F32, name="scaled%d" % first)
            nc.scalar.activation(scaled[:], placed2[:, first : first + width], ACT.Copy, scale=factor[:])
            return scaled

        partials = []
        back = []
        for step in range(len(TURN_WIDTHS) + TURN_LAG):
            if step < len(SIDE_WIDTHS):
                first, width = sum(SIDE_WIDTHS[:step]), SIDE_WIDTHS[step]
                scaled = scale(first, width)
                partial = keep.tile([P, width], F32, name="partial%d" % step)
                nc.gpsimd.tensor_tensor(partial[:], scaled[:], before[:, first : first + width], ALU.add)
                partials.append(partial)
            if step >= TURN_LAG:
                r = step - TURN_LAG
                width = TURN_WIDTHS[r]
                summed = keep.tile([P, width], F32, name="summed%d" % r)
                nc.scalar.copy(out=summed[:], in_=turned[r][:])
                bank = psum.tile([P, width], F32, name="back%d" % r, tag="bank%d" % (len(TURN_WIDTHS) + r))
                for j in range(width // P):
                    nc.tensor.transpose(bank[:, j * P : (j + 1) * P], summed[:, j * P : (j + 1) * P], identity[:])
                back.append(bank)
            if step < len(TURN_WIDTHS):
                width = TURN_WIDTHS[step]
                scaled = scale(turn_starts[step], width)
                for j in range(width // P):
                    nc.tensor.matmul(
                        turned[step][:, j * P : (j + 1) * P],
                        scaled[:, j * P : (j + 1) * P],
                        identity[:],
                        start=False,
                        stop=(j == width // P - 1),
                        is_transpose=True,
                    )
        for b, width in enumerate(SIDE_WIDTHS):
            finish(sum(SIDE_WIDTHS[:b]), width, partials[b][:])
        for r, width in enumerate(TURN_WIDTHS):
            finish(turn_starts[r], width, back[r][:])
